import numpy as np, ml_dtypes
CORES = [0,4,8,12,16,20,24,28,32,36,40,44,48,52,56,60,64,68,72,76,80,84,88,92,96,100,104,108,112,116,120,124,128,132,136,140,144,148,152,156,160,164,168,172,176,180,184,188,192,196,200,204,208,212,216,220,224,228,232,236,240,244,248,252]
N = 64
WINDOW = 4
def setup_inputs(rng):
    return {"q": rng.standard_normal((N, 128, 128), dtype=np.float32).astype(ml_dtypes.bfloat16), "k": rng.standard_normal((N, 128, 128), dtype=np.float32).astype(ml_dtypes.bfloat16), "v": rng.standard_normal((N, 128, 128), dtype=np.float32).astype(ml_dtypes.bfloat16)}
def reference(q, k, v):
    Q, K, V = q.astype(np.float64), k.astype(np.float64), v.astype(np.float64)
    y = np.zeros((N, 128, 128))
    for r in range(N):
        for j in [(r - d) % N for d in range(WINDOW)]:
            y[r] += V[j].T @ np.maximum(K[j].T @ Q[r], 0.0)
    return {"y": y.astype(ml_dtypes.bfloat16 if q.dtype != np.float64 else np.float64)}

@@ -1,0 +1,138 @@
+from concourse.bass import DstId, RemoteDMATransfer
+from concourse.mybir import AluOpType
+
+RANK_A, BLK1, PORT_K, BLK3, RANK_B, BLK2, PORT_V = 0, 1, 2, 3, 4, 5, 6
+E = 4
+M0, M1, M2 = 0x00F, 0x0F0, 0xF00
+
+SCRATCH = {
+    "two": ("sbuf", [128, 256], "bfloat16"),
+    "kb": ("sbuf", [128, 128], "bfloat16"),
+    "vb": ("sbuf", [128, 128], "bfloat16"),
+    "zero": ("sbuf", [128, 256], "float32"),
+    "s_ps": ("psum", [128, 512], "float32"),
+    "o_ps": ("psum", [128, 512], "float32"),
+    "s_sb": ("sbuf", [128, 256], "bfloat16"),
+    "o_sb": ("sbuf", [128, 256], "bfloat16"),
+    "part": ("sbuf", [128, 384], "bfloat16"),
+    "acc": ("sbuf", [128, 256], "float32"),
+    "y_sb": ("sbuf", [128, 128], "bfloat16"),
+}
+SEMAPHORES = [
+    "ld_q", "ld_k", "ld_v", "stored",
+    "sent",
+    "h_in",
+    "qa_in", "qb_in", "k_in", "v_in",
+    "p0_in", "p1_in", "p2_in",
+    "z_done", "s_done", "r_done", "o_done", "c_done", "a_done",
+]
+
+A = slice(0, 128)
+B = slice(128, 256)
+
+
+def work_block(g, T, cols, q_ready, k_ready, v_ready):
+    s = T.sem
+    g.vector.memset(T.zero[:, cols], 0.0).then_inc(s.z_done, 1)
+    for sem, n in q_ready + [k_ready]:
+        g.tensor.wait_ge(sem, n)
+    g.tensor.matmul(T.s_ps[:, cols], T.kb[:], T.two[:, cols], start=True, stop=True).then_inc(s.s_done, 1)
+    g.vector.wait_ge(s.z_done, 1)
+    g.vector.wait_ge(s.s_done, 1)
+    g.vector.tensor_tensor(T.s_sb[:, cols], T.s_ps[:, cols], T.zero[:, cols], AluOpType.max).then_inc(s.r_done, 1)
+    g.tensor.wait_ge(s.r_done, 1)
+    g.tensor.wait_ge(v_ready[0], v_ready[1])
+    g.tensor.matmul(T.o_ps[:, cols], T.vb[:], T.s_sb[:, cols], start=True, stop=True).then_inc(s.o_done, 1)
+    g.vector.wait_ge(s.o_done, 1)
+
+
+def sum_and_store(g, T, own, order):
+    s = T.sem
+    landed = [s.p0_in, s.p1_in, s.p2_in]
+    terms = [T.o_ps[:, own], T.acc[:, A], T.acc[:, B], T.y_sb[:]]
+    for i, slot in enumerate(order):
+        if i:
+            g.vector.wait_ge(s.a_done, i)
+        g.vector.wait_ge(landed[slot], E)
+        g.vector.tensor_tensor(terms[i + 1], terms[i], T.part[:, slot * 128:(slot + 1) * 128],
+                               AluOpType.add).then_inc(s.a_done, 1)
+    g.wait_ge(s.a_done, 3)
+    g.dma_start(T.y[:], T.y_sb[:]).then_inc(s.stored, 16)
+    g.wait_ge(s.stored, 16)
+
+
+def rank_program(g, core, T, topo):
+    chips = len(T.cores) // 2
+    chip, me = core // 8, core % 8
+    s = T.sem
+
+    def to(local, ahead=0):
+        rid, pid = topo.addr(((chip + ahead) % chips) * 8 + local, core)
+        return DstId(rid=rid, pnc=pid)
+
+    def one(dst_core, mask, sem, src, dst):
+        return RemoteDMATransfer(dst_ids=[dst_core], dma_engine_mask=mask, remote_sem=sem, src=src, dst=dst)
+
+    if me in (RANK_A, RANK_B):
+        mine = A if me == RANK_A else B
+        g.dma_start(T.kb[:], T.k[:]).then_inc(s.ld_k, 16)
+        g.dma_start(T.two[:, mine], T.q[:]).then_inc(s.ld_q, 16)
+        g.dma_start(T.vb[:], T.v[:]).then_inc(s.ld_v, 16)
+        g.wait_ge(s.ld_k, 16)
+        g.wait_ge(s.ld_q, 16)
+        g.wait_ge(s.ld_v, 16)
+        if me == RANK_A:
+            q_out = one(to(BLK1), M2, s.qa_in, T.two[:, A], T.two[:, A])
+        else:
+            q_out = RemoteDMATransfer(dst_ids=[to(RANK_A), to(BLK2)], dma_engine_mask=M2, remote_sem=s.qb_in,
+                                      srcs=[T.two[:, B]], dsts=[T.two[:, B], T.two[:, B]])
+        g.remote_dma_fused([one(to(PORT_K), M0, s.h_in, T.kb[:], T.two[:, mine]),
+                            one(to(PORT_V), M1, s.h_in, T.vb[:], T.two[:, mine]),
+                            q_out], local_sem=s.sent)
+        if me == RANK_A:
+            work_block(g, T, slice(0, 256), [(s.ld_q, 16), (s.qb_in, E)], (s.ld_k, 16), (s.ld_v, 16))
+            g.vector.tensor_copy(T.o_sb[:, B], T.o_ps[:, B]).then_inc(s.c_done, 1)
+            g.wait_ge(s.c_done, 1)
+            d = to(RANK_B)
+            g.remote_dma(T.part[:, 256:384], T.o_sb[:, B], s.p2_in, s.sent, d.pnc, d.rid, M0)
+            sum_and_store(g, T, A, [0, 1, 2])
+            g.wait_ge(s.sent, 4 * E)
+        else:
+            work_block(g, T, B, [(s.ld_q, 16)], (s.ld_k, 16), (s.ld_v, 16))
+            sum_and_store(g, T, B, [2, 0, 1])
+            g.wait_ge(s.sent, 3 * E)
+
+    elif me in (PORT_K, PORT_V):
+        land, sem = (T.kb, s.k_in) if me == PORT_K else (T.vb, s.v_in)
+        g.wait_ge(s.h_in, 2 * E)
+        g.remote_dma_fused([one(to(BLK2, 1), M0, sem, T.two[:, A], land[:]),
+                            RemoteDMATransfer(dst_ids=[to(BLK1, 1), to(BLK3, 2)], dma_engine_mask=M1, remote_sem=sem,
+                                              srcs=[T.two[:, B]], dsts=[land[:], land[:]])], local_sem=s.sent)
+        g.wait_ge(s.sent, 2 * E)
+
+    elif me in (BLK1, BLK2):
+        if me == BLK1:
+            g.wait_ge(s.qa_in, E)
+            g.remote_dma_fused([RemoteDMATransfer(dst_ids=[to(BLK2), to(BLK3)], dma_engine_mask=M0,
+                                                  remote_sem=s.qa_in, srcs=[T.two[:, A]],
+                                                  dsts=[T.two[:, A], T.two[:, A]])], local_sem=s.sent)
+            slot, landed = T.part[:, 0:128], s.p0_in
+        else:
+            g.wait_ge(s.qb_in, E)
+            d = to(BLK1)
+            g.remote_dma(T.two[:, B], T.two[:, B], s.qb_in, s.sent, d.pnc, d.rid, M0)
+            slot, landed = T.part[:, 128:256], s.p1_in
+        work_block(g, T, slice(0, 256), [(s.qa_in, E), (s.qb_in, E)], (s.k_in, E), (s.v_in, E))
+        g.vector.tensor_copy(T.o_sb[:], T.o_ps[:, 0:256]).then_inc(s.c_done, 1)
+        g.wait_ge(s.c_done, 1)
+        g.remote_dma_fused([one(to(RANK_A), M0, landed, T.o_sb[:, A], slot),
+                            one(to(RANK_B), M1, landed, T.o_sb[:, B], slot)], local_sem=s.sent)
+        g.wait_ge(s.sent, 3 * E)
+
+    elif me == BLK3:
+        work_block(g, T, A, [(s.qa_in, E)], (s.k_in, E), (s.v_in, E))
+        g.vector.tensor_copy(T.o_sb[:, A], T.o_ps[:, A]).then_inc(s.c_done, 1)
+        g.wait_ge(s.c_done, 1)
+        d = to(RANK_A)
+        g.remote_dma(T.part[:, 256:384], T.o_sb[:, A], s.p2_in, s.sent, d.pnc, d.rid, M0)
+        g.wait_ge(s.sent, E)

@@ -1,14 +1,14 @@
 from concourse.bass import DstId, RemoteDMATransfer
 from concourse.mybir import AluOpType
 
-RANK_A, BLK1, PORT_K, BLK3, RANK_B, BLK2, PORT_V = 0, 1, 2, 3, 4, 5, 6
-E = 4
-M0, M1, M2 = 0x00F, 0x0F0, 0xF00
+RANK_A, BLK1, PORT_A, BLK3, RANK_B, BLK2, PORT_B, SPREAD = 0, 1, 2, 3, 4, 5, 6, 7
+
+WIDE, LO, HI, UP0, UP1 = 0x00FF, 0x000F, 0x00F0, 0x0F00, 0xF000
+E8, E4 = 8, 4
 
 SCRATCH = {
-    "two": ("sbuf", [128, 256], "bfloat16"),
-    "kb": ("sbuf", [128, 128], "bfloat16"),
-    "vb": ("sbuf", [128, 128], "bfloat16"),
+    "qq": ("sbuf", [128, 256], "bfloat16"),
+    "kv": ("sbuf", [128, 256], "bfloat16"),
     "zero": ("sbuf", [128, 256], "float32"),
     "s_ps": ("psum", [128, 512], "float32"),
     "o_ps": ("psum", [128, 512], "float32"),
@@ -21,29 +21,37 @@ SCRATCH = {
 SEMAPHORES = [
     "ld_q", "ld_k", "ld_v", "stored",
     "sent",
-    "h_in",
-    "qa_in", "qb_in", "k_in", "v_in",
+    "kv_in", "k_in", "v_in",
+    "qa_in", "qb_in",
+    "kf_in",
     "p0_in", "p1_in", "p2_in",
     "z_done", "s_done", "r_done", "o_done", "c_done", "a_done",
 ]
 
 A = slice(0, 128)
 B = slice(128, 256)
+AB = slice(0, 256)
 
 
-def work_block(g, T, cols, q_ready, k_ready, v_ready):
+def work_block(g, T, cols, ready_s, ready_o):
     s = T.sem
     g.vector.memset(T.zero[:, cols], 0.0).then_inc(s.z_done, 1)
-    for sem, n in q_ready + [k_ready]:
+    for sem, n in ready_s:
         g.tensor.wait_ge(sem, n)
-    g.tensor.matmul(T.s_ps[:, cols], T.kb[:], T.two[:, cols], start=True, stop=True).then_inc(s.s_done, 1)
+    g.tensor.matmul(T.s_ps[:, cols], T.kv[:, A], T.qq[:, cols], start=True, stop=True).then_inc(s.s_done, 1)
     g.vector.wait_ge(s.z_done, 1)
     g.vector.wait_ge(s.s_done, 1)
     g.vector.tensor_tensor(T.s_sb[:, cols], T.s_ps[:, cols], T.zero[:, cols], AluOpType.max).then_inc(s.r_done, 1)
     g.tensor.wait_ge(s.r_done, 1)
-    g.tensor.wait_ge(v_ready[0], v_ready[1])
-    g.tensor.matmul(T.o_ps[:, cols], T.vb[:], T.s_sb[:, cols], start=True, stop=True).then_inc(s.o_done, 1)
+    for sem, n in ready_o:
+        g.tensor.wait_ge(sem, n)
+    g.tensor.matmul(T.o_ps[:, cols], T.kv[:, B], T.s_sb[:, cols], start=True, stop=True).then_inc(s.o_done, 1)
     g.vector.wait_ge(s.o_done, 1)
+
+
+def round_for_sending(g, T, cols):
+    g.vector.tensor_copy(T.o_sb[:, cols], T.o_ps[:, cols]).then_inc(T.sem.c_done, 1)
+    g.wait_ge(T.sem.c_done, 1)
 
 
 def sum_and_store(g, T, own, order):
@@ -53,7 +61,7 @@ def sum_and_store(g, T, own, order):
     for i, slot in enumerate(order):
         if i:
             g.vector.wait_ge(s.a_done, i)
-        g.vector.wait_ge(landed[slot], E)
+        g.vector.wait_ge(landed[slot], E4)
         g.vector.tensor_tensor(terms[i + 1], terms[i], T.part[:, slot * 128:(slot + 1) * 128],
                                AluOpType.add).then_inc(s.a_done, 1)
     g.wait_ge(s.a_done, 3)
@@ -65,74 +73,78 @@ def rank_program(g, core, T, topo):
     chips = len(T.cores) // 2
     chip, me = core // 8, core % 8
     s = T.sem
+    slot0, slot1, slot2 = T.part[:, 0:128], T.part[:, 128:256], T.part[:, 256:384]
 
     def to(local, ahead=0):
         rid, pid = topo.addr(((chip + ahead) % chips) * 8 + local, core)
         return DstId(rid=rid, pnc=pid)
 
-    def one(dst_core, mask, sem, src, dst):
-        return RemoteDMATransfer(dst_ids=[dst_core], dma_engine_mask=mask, remote_sem=sem, src=src, dst=dst)
+    def write(dst_core, mask, sem, src, dst):
+        g.remote_dma(dst, src, sem, s.sent, dst_core.pnc, dst_core.rid, mask)
+
+    def copies(dst_cores, mask, sem, src, dst):
+        return RemoteDMATransfer(dst_ids=dst_cores, dma_engine_mask=mask, remote_sem=sem,
+                                 srcs=[src], dsts=[dst] * len(dst_cores))
 
     if me in (RANK_A, RANK_B):
         mine = A if me == RANK_A else B
-        g.dma_start(T.kb[:], T.k[:]).then_inc(s.ld_k, 16)
-        g.dma_start(T.two[:, mine], T.q[:]).then_inc(s.ld_q, 16)
-        g.dma_start(T.vb[:], T.v[:]).then_inc(s.ld_v, 16)
+        g.dma_start(T.kv[:, A], T.k[:]).then_inc(s.ld_k, 16)
+        g.dma_start(T.kv[:, B], T.v[:]).then_inc(s.ld_v, 16)
+        g.dma_start(T.qq[:, mine], T.q[:]).then_inc(s.ld_q, 16)
         g.wait_ge(s.ld_k, 16)
-        g.wait_ge(s.ld_q, 16)
         g.wait_ge(s.ld_v, 16)
+        write(to(PORT_A if me == RANK_A else PORT_B), WIDE, s.kv_in, T.kv[:], T.kv[:])
+        g.wait_ge(s.ld_q, 16)
         if me == RANK_A:
-            q_out = one(to(BLK1), M2, s.qa_in, T.two[:, A], T.two[:, A])
+            g.remote_dma_fused([copies([to(BLK1), to(BLK2)], UP0, s.qa_in, T.qq[:, A], T.qq[:, A])], local_sem=s.sent)
+            sent = E8 + E4
+            order = [0, 1, 2]
         else:
-            q_out = RemoteDMATransfer(dst_ids=[to(RANK_A), to(BLK2)], dma_engine_mask=M2, remote_sem=s.qb_in,
-                                      srcs=[T.two[:, B]], dsts=[T.two[:, B], T.two[:, B]])
-        g.remote_dma_fused([one(to(PORT_K), M0, s.h_in, T.kb[:], T.two[:, mine]),
-                            one(to(PORT_V), M1, s.h_in, T.vb[:], T.two[:, mine]),
-                            q_out], local_sem=s.sent)
-        if me == RANK_A:
-            work_block(g, T, slice(0, 256), [(s.ld_q, 16), (s.qb_in, E)], (s.ld_k, 16), (s.ld_v, 16))
-            g.vector.tensor_copy(T.o_sb[:, B], T.o_ps[:, B]).then_inc(s.c_done, 1)
-            g.wait_ge(s.c_done, 1)
-            d = to(RANK_B)
-            g.remote_dma(T.part[:, 256:384], T.o_sb[:, B], s.p2_in, s.sent, d.pnc, d.rid, M0)
-            sum_and_store(g, T, A, [0, 1, 2])
-            g.wait_ge(s.sent, 4 * E)
-        else:
-            work_block(g, T, B, [(s.ld_q, 16)], (s.ld_k, 16), (s.ld_v, 16))
-            sum_and_store(g, T, B, [2, 0, 1])
-            g.wait_ge(s.sent, 3 * E)
+            g.remote_dma_fused([copies([to(BLK3)], UP0, s.kf_in, T.kv[:, A], T.qq[:, B]),
+                                copies([to(SPREAD)], UP1, s.qb_in, T.qq[:, B], T.qq[:, B])], local_sem=s.sent)
+            sent = E8 + E4 + E4
+            order = [2, 0, 1]
+        work_block(g, T, mine, [(s.ld_q, 16), (s.ld_k, 16)], [(s.ld_v, 16)])
+        sum_and_store(g, T, mine, order)
+        g.wait_ge(s.sent, sent)
 
-    elif me in (PORT_K, PORT_V):
-        land, sem = (T.kb, s.k_in) if me == PORT_K else (T.vb, s.v_in)
-        g.wait_ge(s.h_in, 2 * E)
-        g.remote_dma_fused([one(to(BLK2, 1), M0, sem, T.two[:, A], land[:]),
-                            RemoteDMATransfer(dst_ids=[to(BLK1, 1), to(BLK3, 2)], dma_engine_mask=M1, remote_sem=sem,
-                                              srcs=[T.two[:, B]], dsts=[land[:], land[:]])], local_sem=s.sent)
-        g.wait_ge(s.sent, 2 * E)
+    elif me == PORT_A:
+        g.wait_ge(s.kv_in, E8)
+        write(to(BLK2, 1), WIDE, s.kv_in, T.kv[:], T.kv[:])
+        work_block(g, T, B, [(s.qb_in, E4), (s.kv_in, E8)], [])
+        round_for_sending(g, T, B)
+        write(to(RANK_B), LO, s.p2_in, T.o_sb[:, B], slot2)
+        g.wait_ge(s.sent, E8 + E4)
+
+    elif me == PORT_B:
+        g.wait_ge(s.kv_in, E8)
+        write(to(BLK1, 1), WIDE, s.kv_in, T.kv[:], T.kv[:])
+        write(to(BLK3, 2), WIDE, s.v_in, T.kv[:, B], T.kv[:, B])
+        g.wait_ge(s.sent, E8 + E8)
+
+    elif me == SPREAD:
+        g.wait_ge(s.qb_in, E4)
+        g.remote_dma_fused([copies([to(BLK1), to(BLK2), to(PORT_A)], LO, s.qb_in, T.qq[:, B], T.qq[:, B])],
+                           local_sem=s.sent)
+        g.wait_ge(s.sent, E4)
 
     elif me in (BLK1, BLK2):
+        sent = 0
         if me == BLK1:
-            g.wait_ge(s.qa_in, E)
-            g.remote_dma_fused([RemoteDMATransfer(dst_ids=[to(BLK2), to(BLK3)], dma_engine_mask=M0,
-                                                  remote_sem=s.qa_in, srcs=[T.two[:, A]],
-                                                  dsts=[T.two[:, A], T.two[:, A]])], local_sem=s.sent)
-            slot, landed = T.part[:, 0:128], s.p0_in
-        else:
-            g.wait_ge(s.qb_in, E)
-            d = to(BLK1)
-            g.remote_dma(T.two[:, B], T.two[:, B], s.qb_in, s.sent, d.pnc, d.rid, M0)
-            slot, landed = T.part[:, 128:256], s.p1_in
-        work_block(g, T, slice(0, 256), [(s.qa_in, E), (s.qb_in, E)], (s.k_in, E), (s.v_in, E))
-        g.vector.tensor_copy(T.o_sb[:], T.o_ps[:, 0:256]).then_inc(s.c_done, 1)
-        g.wait_ge(s.c_done, 1)
-        g.remote_dma_fused([one(to(RANK_A), M0, landed, T.o_sb[:, A], slot),
-                            one(to(RANK_B), M1, landed, T.o_sb[:, B], slot)], local_sem=s.sent)
-        g.wait_ge(s.sent, 3 * E)
+            g.wait_ge(s.qa_in, E4)
+            write(to(BLK3), LO, s.qa_in, T.qq[:, A], T.qq[:, A])
+            sent = E4
+        slot, landed = (slot0, s.p0_in) if me == BLK1 else (slot1, s.p1_in)
+        work_block(g, T, AB, [(s.qa_in, E4), (s.qb_in, E4), (s.kv_in, E8)], [])
+        round_for_sending(g, T, AB)
+        g.remote_dma_fused([copies([to(RANK_A)], LO, landed, T.o_sb[:, A], slot),
+                            copies([to(RANK_B)], HI, landed, T.o_sb[:, B], slot)], local_sem=s.sent)
+        g.wait_ge(s.sent, sent + E4 + E4)
 
     elif me == BLK3:
-        work_block(g, T, A, [(s.qa_in, E)], (s.k_in, E), (s.v_in, E))
-        g.vector.tensor_copy(T.o_sb[:, A], T.o_ps[:, A]).then_inc(s.c_done, 1)
-        g.wait_ge(s.c_done, 1)
-        d = to(RANK_A)
-        g.remote_dma(T.part[:, 256:384], T.o_sb[:, A], s.p2_in, s.sent, d.pnc, d.rid, M0)
-        g.wait_ge(s.sent, E)
+        g.wait_ge(s.kf_in, E4)
+        write(to(BLK3, 2), WIDE, s.k_in, T.qq[:, B], T.kv[:, A])
+        work_block(g, T, A, [(s.qa_in, E4), (s.k_in, E8)], [(s.v_in, E8)])
+        round_for_sending(g, T, A)
+        write(to(RANK_A), LO, s.p2_in, T.o_sb[:, A], slot2)
+        g.wait_ge(s.sent, E8 + E4)

from concourse.bass import DstId, RemoteDMATransfer
from concourse.mybir import AluOpType

RANK_A, BLK1, PORT_A, BLK3, RANK_B, BLK2, PORT_B, SPREAD = 0, 1, 2, 3, 4, 5, 6, 7

WIDE, LO, HI, UP0, UP1 = 0x00FF, 0x000F, 0x00F0, 0x0F00, 0xF000
E8, E4 = 8, 4

SCRATCH = {
    "qq": ("sbuf", [128, 256], "bfloat16"),
    "kv": ("sbuf", [128, 256], "bfloat16"),
    "zero": ("sbuf", [128, 256], "float32"),
    "s_ps": ("psum", [128, 512], "float32"),
    "o_ps": ("psum", [128, 512], "float32"),
    "s_sb": ("sbuf", [128, 256], "bfloat16"),
    "o_sb": ("sbuf", [128, 256], "bfloat16"),
    "part": ("sbuf", [128, 384], "bfloat16"),
    "acc": ("sbuf", [128, 256], "float32"),
    "y_sb": ("sbuf", [128, 128], "bfloat16"),
}
SEMAPHORES = [
    "ld_q", "ld_k", "ld_v", "stored",
    "sent",
    "kv_in", "k_in", "v_in",
    "qa_in", "qb_in",
    "kf_in",
    "p0_in", "p1_in", "p2_in",
    "z_done", "s_done", "r_done", "o_done", "c_done", "a_done",
]

A = slice(0, 128)
B = slice(128, 256)
AB = slice(0, 256)


def work_block(g, T, cols, ready_s, ready_o):
    s = T.sem
    g.vector.memset(T.zero[:, cols], 0.0).then_inc(s.z_done, 1)
    for sem, n in ready_s:
        g.tensor.wait_ge(sem, n)
    g.tensor.matmul(T.s_ps[:, cols], T.kv[:, A], T.qq[:, cols], start=True, stop=True).then_inc(s.s_done, 1)
    g.vector.wait_ge(s.z_done, 1)
    g.vector.wait_ge(s.s_done, 1)
    g.vector.tensor_tensor(T.s_sb[:, cols], T.s_ps[:, cols], T.zero[:, cols], AluOpType.max).then_inc(s.r_done, 1)
    g.tensor.wait_ge(s.r_done, 1)
    for sem, n in ready_o:
        g.tensor.wait_ge(sem, n)
    g.tensor.matmul(T.o_ps[:, cols], T.kv[:, B], T.s_sb[:, cols], start=True, stop=True).then_inc(s.o_done, 1)
    g.vector.wait_ge(s.o_done, 1)


def round_for_sending(g, T, cols):
    g.vector.tensor_copy(T.o_sb[:, cols], T.o_ps[:, cols]).then_inc(T.sem.c_done, 1)
    g.wait_ge(T.sem.c_done, 1)


def sum_and_store(g, T, own, order):
    s = T.sem
    landed = [s.p0_in, s.p1_in, s.p2_in]
    terms = [T.o_ps[:, own], T.acc[:, A], T.acc[:, B], T.y_sb[:]]
    for i, slot in enumerate(order):
        if i:
            g.vector.wait_ge(s.a_done, i)
        g.vector.wait_ge(landed[slot], E4)
        g.vector.tensor_tensor(terms[i + 1], terms[i], T.part[:, slot * 128:(slot + 1) * 128],
                               AluOpType.add).then_inc(s.a_done, 1)
    g.wait_ge(s.a_done, 3)
    g.dma_start(T.y[:], T.y_sb[:]).then_inc(s.stored, 16)
    g.wait_ge(s.stored, 16)


def rank_program(g, core, T, topo):
    chips = len(T.cores) // 2
    chip, me = core // 8, core % 8
    s = T.sem
    slot0, slot1, slot2 = T.part[:, 0:128], T.part[:, 128:256], T.part[:, 256:384]

    def to(local, ahead=0):
        rid, pid = topo.addr(((chip + ahead) % chips) * 8 + local, core)
        return DstId(rid=rid, pnc=pid)

    def write(dst_core, mask, sem, src, dst):
        g.remote_dma(dst, src, sem, s.sent, dst_core.pnc, dst_core.rid, mask)

    def copies(dst_cores, mask, sem, src, dst):
        return RemoteDMATransfer(dst_ids=dst_cores, dma_engine_mask=mask, remote_sem=sem,
                                 srcs=[src], dsts=[dst] * len(dst_cores))

    if me in (RANK_A, RANK_B):
        mine = A if me == RANK_A else B
        g.dma_start(T.kv[:, A], T.k[:]).then_inc(s.ld_k, 16)
        g.dma_start(T.kv[:, B], T.v[:]).then_inc(s.ld_v, 16)
        g.dma_start(T.qq[:, mine], T.q[:]).then_inc(s.ld_q, 16)
        g.wait_ge(s.ld_k, 16)
        g.wait_ge(s.ld_v, 16)
        write(to(PORT_A if me == RANK_A else PORT_B), WIDE, s.kv_in, T.kv[:], T.kv[:])
        g.wait_ge(s.ld_q, 16)
        if me == RANK_A:
            g.remote_dma_fused([copies([to(BLK1), to(BLK2)], UP0, s.qa_in, T.qq[:, A], T.qq[:, A])], local_sem=s.sent)
            sent = E8 + E4
            order = [0, 1, 2]
        else:
            g.remote_dma_fused([copies([to(BLK3)], UP0, s.kf_in, T.kv[:, A], T.qq[:, B]),
                                copies([to(SPREAD)], UP1, s.qb_in, T.qq[:, B], T.qq[:, B])], local_sem=s.sent)
            sent = E8 + E4 + E4
            order = [2, 0, 1]
        work_block(g, T, mine, [(s.ld_q, 16), (s.ld_k, 16)], [(s.ld_v, 16)])
        sum_and_store(g, T, mine, order)
        g.wait_ge(s.sent, sent)

    elif me == PORT_A:
        g.wait_ge(s.kv_in, E8)
        write(to(BLK2, 1), WIDE, s.kv_in, T.kv[:], T.kv[:])
        work_block(g, T, B, [(s.qb_in, E4), (s.kv_in, E8)], [])
        round_for_sending(g, T, B)
        write(to(RANK_B), LO, s.p2_in, T.o_sb[:, B], slot2)
        g.wait_ge(s.sent, E8 + E4)

    elif me == PORT_B:
        g.wait_ge(s.kv_in, E8)
        write(to(BLK1, 1), WIDE, s.kv_in, T.kv[:], T.kv[:])
        write(to(BLK3, 2), WIDE, s.v_in, T.kv[:, B], T.kv[:, B])
        g.wait_ge(s.sent, E8 + E8)

    elif me == SPREAD:
        g.wait_ge(s.qb_in, E4)
        g.remote_dma_fused([copies([to(BLK1), to(BLK2), to(PORT_A)], LO, s.qb_in, T.qq[:, B], T.qq[:, B])],
                           local_sem=s.sent)
        g.wait_ge(s.sent, E4)

    elif me in (BLK1, BLK2):
        sent = 0
        if me == BLK1:
            g.wait_ge(s.qa_in, E4)
            write(to(BLK3), LO, s.qa_in, T.qq[:, A], T.qq[:, A])
            sent = E4
        slot, landed = (slot0, s.p0_in) if me == BLK1 else (slot1, s.p1_in)
        work_block(g, T, AB, [(s.qa_in, E4), (s.qb_in, E4), (s.kv_in, E8)], [])
        round_for_sending(g, T, AB)
        g.remote_dma_fused([copies([to(RANK_A)], LO, landed, T.o_sb[:, A], slot),
                            copies([to(RANK_B)], HI, landed, T.o_sb[:, B], slot)], local_sem=s.sent)
        g.wait_ge(s.sent, sent + E4 + E4)

    elif me == BLK3:
        g.wait_ge(s.kf_in, E4)
        write(to(BLK3, 2), WIDE, s.k_in, T.qq[:, B], T.kv[:, A])
        work_block(g, T, A, [(s.qa_in, E4), (s.k_in, E8)], [(s.v_in, E8)])
        round_for_sending(g, T, A)
        write(to(RANK_A), LO, s.p2_in, T.o_sb[:, A], slot2)
        g.wait_ge(s.sent, E8 + E4)
